import numpy as np
import ml_dtypes


def mxq(x, axis, fmt="e4m3"):
    dtype, down = {"e4m3": (ml_dtypes.float8_e4m3fn, 7), "e5m2": (ml_dtypes.float8_e5m2, 14)}[fmt]
    v = np.moveaxis(np.asarray(x, np.float32).astype(ml_dtypes.bfloat16).astype(np.float64), axis, -1)
    blocks = v.reshape(v.shape[:-1] + (-1, 32))
    amax = np.abs(blocks).max(-1, keepdims=True)
    byte = np.maximum(np.where(amax > 0, np.frexp(amax)[1] - 1 + 127, 0) - down, 1)
    scale = np.exp2(byte - 127.0)
    codes = (blocks / scale).astype(np.float32).astype(dtype).astype(np.float64)
    return np.moveaxis((codes * scale).reshape(v.shape), -1, axis)


WIDE = False


def mx_kscale(k):
    if not WIDE:
        return np.ones(k)
    levels = np.array([10, -10, 5, -5, 0])
    if k % 512:
        return np.exp2(np.random.permutation(np.resize(levels, k // 32))).repeat(32)
    a = np.empty((k // 512, 16))
    for p in range(k // 512):
        a[p, :8] = np.random.permutation(np.resize(levels, 8))
        for g in range(8):
            far = levels[np.abs(levels - a[p, g]) >= 10]
            a[p, g + 8] = far[np.random.randint(len(far))]
    return np.exp2(a.ravel()).repeat(32)


def f64(x):
    return np.asarray(x).astype(np.float64)


def striped(idx):
    return np.tile(idx.reshape(-1, 16).T, (8, 1)).astype(np.uint16)


def unstriped(offs):
    return offs[:16].T.reshape(-1).astype(np.int64)


E2M1 = np.array([0.0, 0.5, 1.0, 1.5, 2.0, 3.0, 4.0, 6.0, -0.0, -0.5, -1.0, -1.5, -2.0, -3.0, -4.0, -6.0])


def pack_weight(w, fmt):
    k, n = w.shape
    w = f64(np.asarray(w, np.float32).astype(ml_dtypes.bfloat16)).reshape(k // 32, 32, n)
    amax = np.abs(w).max(1)
    if fmt == "e4m3":
        byte = np.frexp(amax)[1] - 1 + 127 - 7
    else:
        mant, ex = np.frexp(amax / 6.0)
        byte = np.where(mant > 0.5, ex, ex - 1) + 127
    byte = np.clip(np.where(amax > 0, byte, 1), 1, 254)
    scaled = (w * np.exp2(127.0 - byte)[:, None, :]).reshape(k, n).astype(np.float32)
    by_word = np.ascontiguousarray(scaled.reshape(k // 512, 128, 4, n).transpose(0, 1, 3, 2))
    if fmt == "e4m3":
        words = by_word.astype(ml_dtypes.float8_e4m3fn).view(np.uint8)
    else:
        c = by_word.astype(ml_dtypes.float4_e2m1fn).view(np.uint8) & 0xF
        words = (c[..., 0::2] | (c[..., 1::2] << 4)).reshape(k // 512, 128, 2 * n)
    return np.ascontiguousarray(words), np.ascontiguousarray(byte.astype(np.uint8).reshape(k // 512, 16, n))


def unpack_weight(words, scales, fmt):
    g, _, n = scales.shape
    words = np.ascontiguousarray(words).reshape(g, 128, n, -1)
    if fmt == "e4m3":
        vals = words.view(ml_dtypes.float8_e4m3fn).astype(np.float64)
    else:
        nib = np.empty((g, 128, n, 4), np.uint8)
        nib[..., 0::2] = words & 0xF
        nib[..., 1::2] = words >> 4
        vals = E2M1[nib]
    vals = vals * np.repeat(np.exp2(scales.astype(np.float64) - 127.0), 8, axis=1)[..., None]
    return vals.transpose(0, 1, 3, 2).reshape(g * 512, n)


def pack_table4(v):
    words, scales = pack_weight(v, "e2m1")
    g, t = words.shape[0] // 2, v.shape[1]
    words = words.reshape(g, 2, 128, t, 2).transpose(0, 2, 3, 1, 4)
    return np.concatenate([words.reshape(g, -1), scales.reshape(g, -1)], axis=1)


def unpack_table4(tab):
    g, t = tab.shape[0], tab.shape[1] // 544
    words = tab[:, :512 * t].reshape(g, 128, t, 2, 2).transpose(0, 3, 1, 2, 4).reshape(2 * g, 128, 2 * t)
    return unpack_weight(words, tab[:, 512 * t:].reshape(2 * g, 16, t), "e2m1")


K, M, T, S = 2048, 1024, 512, 256


def setup_inputs():
    n = np.random.standard_normal
    s = mx_kscale(K)[:, None]
    return {
        "tab": pack_table4(n((K, T)) * s),
        "w": (n((K, M)) / np.sqrt(K) / s).astype(np.float32),
        "offs": striped(np.random.permutation(T)[:S]),
    }


def reference(tab, w, offs):
    tab_ = unpack_table4(tab)[:, unstriped(offs)]
    w_ = mxq(f64(w), 0, "e4m3")
    y = tab_.T @ w_
    return y

@@ -1,0 +1,162 @@
+from contextlib import ExitStack
+
+import concourse.mybir as mybir
+
+K, M, T, S = 2048, 1024, 512, 256
+FLOPS = 2 * K * M * S
+
+F32 = mybir.dt.float32
+BF16 = mybir.dt.bfloat16
+I32 = mybir.dt.int32
+U32 = mybir.dt.uint32
+U16 = mybir.dt.uint16
+U8 = mybir.dt.uint8
+FP8X4 = mybir.dt.float8_e4m3fn_x4
+FP4X4 = mybir.dt.float4_e2m1fn_x4
+
+P = 128
+PACK = 4
+K_PASS = P * PACK
+PASSES = K // K_PASS
+PAIRS = PASSES // 2
+J_TILES = S // P
+WORD_BYTES = P * T * 4
+
+GROUPS = ((0, 512), (512, 256), (768, 256))
+PARTS = (((0, 1024),), ((0, 1024),), ((0, 512), (512, 512)))
+PLAN = (
+    (0, 0, 1024),
+    (1, 0, 1024),
+    (2, 0, 1024),
+    (3, 0, 512),
+    (3, 512, 256),
+    (3, 768, 256),
+)
+VECTOR_SHARE = {256: 160, 512: 272, 1024: 512}
+
+
+def tile_list_tab4_tm_none_kernel(tc, tab, w, offs, out):
+    nc = tc.nc
+    with ExitStack() as ctx:
+        keep = ctx.enter_context(tc.tile_pool(name="keep", bufs=1))
+        psum = ctx.enter_context(tc.psum_pool(name="psum", bufs=1))
+
+        offsets = keep.tile([P, S // 16], U16, name="offsets")
+        words = keep.tile([P, PAIRS, T], I32, name="words", align_bytes=64)
+        planes = [keep.tile([P, 2, T], U8, name=f"planes{m}", align_bytes=64) for m in range(PAIRS)]
+        for m in range(PAIRS):
+            nc.vector.memset(planes[m][:].rearrange("p h t -> p (h t)").bitcast(I32), 0)
+
+        nc.sync.dma_start(offsets[:], offs)
+        tab32 = tab.bitcast(I32)
+        nc.sync.dma_start(
+            out=words[:],
+            in_=tab32[:, 0 : WORD_BYTES // 4].rearrange("m (p t) -> p m t", p=P),
+        )
+
+        def load_planes(m):
+            rows = tab32[m, WORD_BYTES // 4 : (WORD_BYTES + 32 * T) // 4].rearrange("(h q t) -> q h t", h=2, q=16)
+            view = planes[m][:].rearrange("p h t -> p (h t)").bitcast(I32).rearrange("p (h t) -> p h t", h=2)
+            for quad in range(4):
+                nc.sync.dma_start(out=view[32 * quad : 32 * quad + 4], in_=rows[4 * quad : 4 * quad + 4])
+
+        load_planes(0)
+        raw = []
+        for step, (a, c0, width) in enumerate(PLAN):
+            if step == 1:
+                load_planes(1)
+            piece = keep.tile([P, PACK, width], F32, name=f"raw{a}_{c0}", align_bytes=64)
+            nc.sync.dma_start(
+                out=piece[:],
+                in_=w[a * K_PASS : (a + 1) * K_PASS, c0 : c0 + width].rearrange("(p j) c -> p j c", j=PACK),
+            )
+            raw.append(piece)
+
+        t_codes = [keep.tile([P, 2, 2 * S], U8, name=f"t_codes{m}", align_bytes=64) for m in range(PAIRS)]
+        t_scales = keep.tile([P, PASSES, S], U8, name="t_scales", align_bytes=64)
+        def gather(m):
+            picked = keep.tile([P, S], U32, name=f"picked{m}", align_bytes=64)
+            nc.vector.tensor_copy(picked[:], words[:, m, :].bitcast(U32).indirect(offsets[:]))
+            nc.vector.tensor_copy(
+                out=t_codes[m][:].rearrange("p h b -> p (h b)").bitcast(U16).rearrange("p (h t) -> p h t", h=2),
+                in_=picked[:].bitcast(U16).rearrange("p (t h) -> p h t", h=2),
+            )
+
+        def gather_scales(m):
+            for h in range(2):
+                nc.vector.tensor_copy(t_scales[:, 2 * m + h, :], planes[m][:, h, :].indirect(offsets[:]))
+
+        gather(0)
+        gather_scales(0)
+        gather(1)
+        grouped = [keep.tile([P, M, PACK], BF16, name=f"grouped{a}", align_bytes=64) for a in range(PASSES)]
+        w_codes = [keep.tile([P, M], U32, name=f"w_codes{a}", align_bytes=64) for a in range(PASSES)]
+        w_scales = [keep.tile([P, M], U8, name=f"w_scales{a}", align_bytes=64) for a in range(PASSES)]
+        acc = {
+            (j, c0): psum.tile([P, width], F32, name=f"acc{j}_{c0}")
+            for c0, width in GROUPS
+            for j in range(J_TILES)
+        }
+
+        def cast(a, c0, width):
+            first, piece = [(f, t) for (b, f, n), t in zip(PLAN, raw) if b == a and f <= c0 < f + n][0]
+            src = piece[:, :, c0 - first : c0 - first + width]
+            share = VECTOR_SHARE[width]
+            dst = grouped[a][:, c0 : c0 + width, :]
+            for copy, cols in ((nc.vector.tensor_copy, slice(0, share)), (nc.scalar.copy, slice(share, width))):
+                copy(
+                    out=dst[:, cols, :].rearrange("p (c i) j -> p c j i", i=4),
+                    in_=src[:, :, cols].rearrange("p j (c i) -> p c j i", i=4),
+                )
+
+        def quantise(a, c0, width):
+            cols = slice(c0, c0 + width)
+            nc.vector.quantize_mx(
+                out=w_codes[a][:, cols].bitcast(FP8X4),
+                scales=w_scales[a][:, cols],
+                in_=grouped[a][:, cols, :].rearrange("p c j -> p (c j)"),
+            )
+
+        def multiply(a, c0, width):
+            step = 512 if width == 512 else 128
+            for j in range(J_TILES):
+                for n in range(0, width, step):
+                    cols = slice(c0 + n, c0 + n + step)
+                    nc.tensor.matmul_mx(
+                        out=acc[j, c0][:, n : n + step],
+                        lhsT=t_codes[a // 2][:, a % 2, 2 * P * j : 2 * P * (j + 1)].bitcast(FP4X4),
+                        lhsT_scale=t_scales[:, a, P * j : P * (j + 1)],
+                        rhs=w_codes[a][:, cols].bitcast(FP8X4),
+                        rhs_scale=w_scales[a][:, cols],
+                        start=(a == 0 and n == 0),
+                        stop=(a == PASSES - 1 and n + step == width),
+                    )
+
+        out_view = out.rearrange("(j p) n -> p j n", p=P)
+
+        def finish(c0, width):
+            result = keep.tile([P, J_TILES, width], F32, name=f"result{c0}", align_bytes=64)
+            if c0 in (0, 768):
+                nc.vector.tensor_copy(out=result[:, 0, :], in_=acc[0, c0][:])
+            else:
+                nc.scalar.copy(out=result[:, 0, :], in_=acc[0, c0][:])
+            nc.scalar.copy(out=result[:, 1, :], in_=acc[1, c0][:])
+            nc.sync.dma_start(out=out_view[:, :, c0 : c0 + width], in_=result[:])
+
+        for a in range(PASSES - 1):
+            if a == 1:
+                gather_scales(1)
+            for c0, width in PARTS[a]:
+                cast(a, c0, width)
+            for c0, width in PARTS[a]:
+                quantise(a, c0, width)
+            for c0, width in GROUPS:
+                multiply(a, c0, width)
+        for g, (c0, width) in enumerate(GROUPS):
+            cast(PASSES - 1, c0, width)
+            quantise(PASSES - 1, c0, width)
+            multiply(PASSES - 1, c0, width)
+            if g >= 1:
+                finish(*GROUPS[g - 1])
+        for g in range(len(GROUPS) - 1, len(GROUPS)):
+            finish(*GROUPS[g])

@@ -22,17 +22,9 @@ PAIRS = PASSES // 2
 J_TILES = S // P
 WORD_BYTES = P * T * 4
 
-GROUPS = ((0, 512), (512, 256), (768, 256))
-PARTS = (((0, 1024),), ((0, 1024),), ((0, 512), (512, 512)))
-PLAN = (
-    (0, 0, 1024),
-    (1, 0, 1024),
-    (2, 0, 1024),
-    (3, 0, 512),
-    (3, 512, 256),
-    (3, 768, 256),
-)
-VECTOR_SHARE = {256: 160, 512: 272, 1024: 512}
+GROUPS = ((0, 256, False), (256, 256, False), (512, 256, False), (768, 128, False), (896, 128, True))
+PLAN = ((0, 0, 1024), (1, 0, 1024), (2, 0, 1024), (3, 0, 512), (3, 512, 256), (3, 768, 256))
+N_STEP = 128
 
 
 def tile_list_tab4_tm_none_kernel(tc, tab, w, offs, out):
@@ -47,12 +39,13 @@ def tile_list_tab4_tm_none_kernel(tc, tab, w, offs, out):
         for m in range(PAIRS):
             nc.vector.memset(planes[m][:].rearrange("p h t -> p (h t)").bitcast(I32), 0)
 
-        nc.sync.dma_start(offsets[:], offs)
         tab32 = tab.bitcast(I32)
-        nc.sync.dma_start(
-            out=words[:],
-            in_=tab32[:, 0 : WORD_BYTES // 4].rearrange("m (p t) -> p m t", p=P),
-        )
+
+        def load_words():
+            nc.sync.dma_start(
+                out=words[:],
+                in_=tab32[:, 0 : WORD_BYTES // 4].rearrange("m (p t) -> p m t", p=P),
+            )
 
         def load_planes(m):
             rows = tab32[m, WORD_BYTES // 4 : (WORD_BYTES + 32 * T) // 4].rearrange("(h q t) -> q h t", h=2, q=16)
@@ -60,20 +53,27 @@ def tile_list_tab4_tm_none_kernel(tc, tab, w, offs, out):
             for quad in range(4):
                 nc.sync.dma_start(out=view[32 * quad : 32 * quad + 4], in_=rows[4 * quad : 4 * quad + 4])
 
-        load_planes(0)
-        raw = []
-        for step, (a, c0, width) in enumerate(PLAN):
-            if step == 1:
-                load_planes(1)
+        raw = {}
+
+        def load_w(a, c0, width):
             piece = keep.tile([P, PACK, width], F32, name=f"raw{a}_{c0}", align_bytes=64)
             nc.sync.dma_start(
                 out=piece[:],
                 in_=w[a * K_PASS : (a + 1) * K_PASS, c0 : c0 + width].rearrange("(p j) c -> p j c", j=PACK),
             )
-            raw.append(piece)
+            raw[a, c0, width] = piece
+
+        nc.sync.dma_start(offsets[:], offs)
+        load_words()
+        load_planes(0)
+        load_w(*PLAN[0])
+        load_planes(1)
+        for piece_at in PLAN[1:]:
+            load_w(*piece_at)
 
         t_codes = [keep.tile([P, 2, 2 * S], U8, name=f"t_codes{m}", align_bytes=64) for m in range(PAIRS)]
         t_scales = keep.tile([P, PASSES, S], U8, name="t_scales", align_bytes=64)
+
         def gather(m):
             picked = keep.tile([P, S], U32, name=f"picked{m}", align_bytes=64)
             nc.vector.tensor_copy(picked[:], words[:, m, :].bitcast(U32).indirect(offsets[:]))
@@ -86,28 +86,24 @@ def tile_list_tab4_tm_none_kernel(tc, tab, w, offs, out):
             for h in range(2):
                 nc.vector.tensor_copy(t_scales[:, 2 * m + h, :], planes[m][:, h, :].indirect(offsets[:]))
 
-        gather(0)
-        gather_scales(0)
-        gather(1)
         grouped = [keep.tile([P, M, PACK], BF16, name=f"grouped{a}", align_bytes=64) for a in range(PASSES)]
         w_codes = [keep.tile([P, M], U32, name=f"w_codes{a}", align_bytes=64) for a in range(PASSES)]
         w_scales = [keep.tile([P, M], U8, name=f"w_scales{a}", align_bytes=64) for a in range(PASSES)]
-        acc = {
-            (j, c0): psum.tile([P, width], F32, name=f"acc{j}_{c0}")
-            for c0, width in GROUPS
-            for j in range(J_TILES)
-        }
+        banks = {}
+        for c0, width, parted in GROUPS:
+            held = [(j,) for j in range(J_TILES)] if parted else [tuple(range(J_TILES))]
+            banks[c0] = [(js, psum.tile([P, len(js), width], F32, name=f"acc{c0}_{js[0]}")) for js in held]
 
-        def cast(a, c0, width):
-            first, piece = [(f, t) for (b, f, n), t in zip(PLAN, raw) if b == a and f <= c0 < f + n][0]
+        def cast(a, c0, width, share):
+            first, piece = [(f, t) for (b, f, n), t in raw.items() if b == a and f <= c0 < f + n][0]
             src = piece[:, :, c0 - first : c0 - first + width]
-            share = VECTOR_SHARE[width]
             dst = grouped[a][:, c0 : c0 + width, :]
             for copy, cols in ((nc.vector.tensor_copy, slice(0, share)), (nc.scalar.copy, slice(share, width))):
-                copy(
-                    out=dst[:, cols, :].rearrange("p (c i) j -> p c j i", i=4),
-                    in_=src[:, :, cols].rearrange("p j (c i) -> p c j i", i=4),
-                )
+                if cols.start < cols.stop:
+                    copy(
+                        out=dst[:, cols, :].rearrange("p (c i) j -> p c j i", i=4),
+                        in_=src[:, :, cols].rearrange("p j (c i) -> p c j i", i=4),
+                    )
 
         def quantise(a, c0, width):
             cols = slice(c0, c0 + width)
@@ -117,46 +113,68 @@ def tile_list_tab4_tm_none_kernel(tc, tab, w, offs, out):
                 in_=grouped[a][:, cols, :].rearrange("p c j -> p (c j)"),
             )
 
-        def multiply(a, c0, width):
-            step = 512 if width == 512 else 128
-            for j in range(J_TILES):
-                for n in range(0, width, step):
-                    cols = slice(c0 + n, c0 + n + step)
-                    nc.tensor.matmul_mx(
-                        out=acc[j, c0][:, n : n + step],
-                        lhsT=t_codes[a // 2][:, a % 2, 2 * P * j : 2 * P * (j + 1)].bitcast(FP4X4),
-                        lhsT_scale=t_scales[:, a, P * j : P * (j + 1)],
-                        rhs=w_codes[a][:, cols].bitcast(FP8X4),
-                        rhs_scale=w_scales[a][:, cols],
-                        start=(a == 0 and n == 0),
-                        stop=(a == PASSES - 1 and n + step == width),
-                    )
+        def multiply(a, g):
+            c0, width, parted = GROUPS[g]
+            step = 512 if width == 512 else N_STEP
+            for js, acc in banks[c0]:
+                for j in js:
+                    for n in range(0, width, step):
+                        cols = slice(c0 + n, c0 + n + step)
+                        nc.tensor.matmul_mx(
+                            out=acc[:, j - js[0], n : n + step],
+                            lhsT=t_codes[a // 2][:, a % 2, 2 * P * j : 2 * P * (j + 1)].bitcast(FP4X4),
+                            lhsT_scale=t_scales[:, a, P * j : P * (j + 1)],
+                            rhs=w_codes[a][:, cols].bitcast(FP8X4),
+                            rhs_scale=w_scales[a][:, cols],
+                            start=(a == 0 and j == js[0] and n == 0),
+                            stop=(a == PASSES - 1 and j == js[-1] and n + step == width),
+                        )
 
         out_view = out.rearrange("(j p) n -> p j n", p=P)
 
-        def finish(c0, width):
+        def finish(g, copies):
+            c0, width, parted = GROUPS[g]
             result = keep.tile([P, J_TILES, width], F32, name=f"result{c0}", align_bytes=64)
-            if c0 in (0, 768):
-                nc.vector.tensor_copy(out=result[:, 0, :], in_=acc[0, c0][:])
-            else:
-                nc.scalar.copy(out=result[:, 0, :], in_=acc[0, c0][:])
-            nc.scalar.copy(out=result[:, 1, :], in_=acc[1, c0][:])
+            for (js, acc), copy in zip(banks[c0], copies):
+                copy(out=result[:, js[0] : js[-1] + 1, :], in_=acc[:])
             nc.sync.dma_start(out=out_view[:, :, c0 : c0 + width], in_=result[:])
 
-        for a in range(PASSES - 1):
+        on_vector, on_scalar = nc.vector.tensor_copy, nc.scalar.copy
+        gather(0)
+        gather_scales(0)
+        gather(1)
+        for a in range(2):
             if a == 1:
                 gather_scales(1)
-            for c0, width in PARTS[a]:
-                cast(a, c0, width)
-            for c0, width in PARTS[a]:
-                quantise(a, c0, width)
-            for c0, width in GROUPS:
-                multiply(a, c0, width)
-        for g, (c0, width) in enumerate(GROUPS):
-            cast(PASSES - 1, c0, width)
-            quantise(PASSES - 1, c0, width)
-            multiply(PASSES - 1, c0, width)
-            if g >= 1:
-                finish(*GROUPS[g - 1])
-        for g in range(len(GROUPS) - 1, len(GROUPS)):
-            finish(*GROUPS[g])
+            cast(a, 0, 1024, 512)
+            quantise(a, 0, 1024)
+            for g in range(len(GROUPS)):
+                multiply(a, g)
+        cast(2, 0, 512, 256)
+        cast(2, 512, 512, 256)
+        quantise(2, 0, 512)
+        multiply(2, 0)
+        multiply(2, 1)
+        cast(3, 0, 256, 144)
+        cast(3, 256, 256, 144)
+        quantise(3, 0, 256)
+        multiply(3, 0)
+        quantise(3, 256, 256)
+        multiply(3, 1)
+        quantise(2, 512, 512)
+        for g in (2, 3, 4):
+            multiply(2, g)
+        cast(3, 512, 256, 160)
+        finish(0, [on_scalar])
+        finish(1, [on_scalar])
+        quantise(3, 512, 256)
+        multiply(3, 2)
+        cast(3, 768, 128, 80)
+        cast(3, 896, 128, 80)
+        quantise(3, 768, 128)
+        multiply(3, 3)
+        quantise(3, 896, 128)
+        multiply(3, 4)
+        finish(2, [on_scalar])
+        finish(3, [on_vector])
+        finish(4, [on_vector, on_scalar])

@@ -22,8 +22,8 @@ PAIRS = PASSES // 2
 J_TILES = S // P
 WORD_BYTES = P * T * 4
 
-GROUPS = ((0, 256, False), (256, 256, False), (512, 256, False), (768, 128, False), (896, 128, True))
-PLAN = ((0, 0, 1024), (1, 0, 1024), (2, 0, 1024), (3, 0, 512), (3, 512, 256), (3, 768, 256))
+GROUPS = ((0, 512, True), (512, 256, False), (768, 128, False), (896, 128, True))
+PLAN = ((0, 0, 1024), (1, 0, 1024), (2, 0, 512), (3, 0, 512), (2, 512, 512), (3, 512, 256), (3, 768, 256))
 N_STEP = 128
 
 
@@ -132,12 +132,16 @@ def tile_list_tab4_tm_none_kernel(tc, tab, w, offs, out):
 
         out_view = out.rearrange("(j p) n -> p j n", p=P)
 
-        def finish(g, copies):
+        def finish(g, copies, spent=None):
             c0, width, parted = GROUPS[g]
-            result = keep.tile([P, J_TILES, width], F32, name=f"result{c0}", align_bytes=64)
+            if spent is None:
+                staged = keep.tile([P, J_TILES, width], F32, name=f"result{c0}", align_bytes=64)
+                result = staged[:]
+            else:
+                result = raw[spent][:, 0:J_TILES, 0:width]
             for (js, acc), copy in zip(banks[c0], copies):
                 copy(out=result[:, js[0] : js[-1] + 1, :], in_=acc[:])
-            nc.sync.dma_start(out=out_view[:, :, c0 : c0 + width], in_=result[:])
+            nc.sync.dma_start(out=out_view[:, :, c0 : c0 + width], in_=result)
 
         on_vector, on_scalar = nc.vector.tensor_copy, nc.scalar.copy
         gather(0)
@@ -146,35 +150,32 @@ def tile_list_tab4_tm_none_kernel(tc, tab, w, offs, out):
         for a in range(2):
             if a == 1:
                 gather_scales(1)
-            cast(a, 0, 1024, 512)
-            quantise(a, 0, 1024)
+            for c0 in (0, 512):
+                cast(a, c0, 512, 240)
+            for c0 in (0, 512):
+                quantise(a, c0, 512)
             for g in range(len(GROUPS)):
                 multiply(a, g)
-        cast(2, 0, 512, 256)
-        cast(2, 512, 512, 256)
+        cast(2, 0, 512, 240)
         quantise(2, 0, 512)
         multiply(2, 0)
-        multiply(2, 1)
-        cast(3, 0, 256, 144)
-        cast(3, 256, 256, 144)
-        quantise(3, 0, 256)
+        cast(3, 0, 512, 288)
+        quantise(3, 0, 512)
         multiply(3, 0)
-        quantise(3, 256, 256)
-        multiply(3, 1)
+        cast(2, 512, 512, 288)
+        finish(0, [on_scalar, on_scalar], (2, 512, 512))
         quantise(2, 512, 512)
-        for g in (2, 3, 4):
+        for g in (1, 2, 3):
             multiply(2, g)
-        cast(3, 512, 256, 160)
-        finish(0, [on_scalar])
-        finish(1, [on_scalar])
+        cast(3, 512, 256, 192)
         quantise(3, 512, 256)
-        multiply(3, 2)
+        multiply(3, 1)
         cast(3, 768, 128, 80)
         cast(3, 896, 128, 80)
         quantise(3, 768, 128)
-        multiply(3, 3)
+        multiply(3, 2)
         quantise(3, 896, 128)
-        multiply(3, 4)
-        finish(2, [on_scalar])
-        finish(3, [on_vector])
-        finish(4, [on_vector, on_scalar])
+        multiply(3, 3)
+        finish(1, [on_scalar])
+        finish(2, [on_vector])
+        finish(3, [on_vector, on_scalar])

@@ -63,8 +63,8 @@ def tile_list_tab4_tm_none_kernel(tc, tab, w, offs, out):
             )
             raw[a, c0, width] = piece
 
-        nc.sync.dma_start(offsets[:], offs)
         load_words()
+        nc.sync.dma_start(offsets[:], offs)
         load_planes(0)
         load_w(*PLAN[0])
         load_planes(1)
@@ -113,12 +113,13 @@ def tile_list_tab4_tm_none_kernel(tc, tab, w, offs, out):
                 in_=grouped[a][:, cols, :].rearrange("p c j -> p (c j)"),
             )
 
-        def multiply(a, g):
+        def multiply(a, g, lo=0, hi=None):
             c0, width, parted = GROUPS[g]
-            step = 512 if width == 512 else N_STEP
+            hi = width if hi is None else hi
+            step = 512 if hi - lo == 512 else N_STEP
             for js, acc in banks[c0]:
                 for j in js:
-                    for n in range(0, width, step):
+                    for n in range(lo, hi, step):
                         cols = slice(c0 + n, c0 + n + step)
                         nc.tensor.matmul_mx(
                             out=acc[:, j - js[0], n : n + step],
@@ -132,16 +133,31 @@ def tile_list_tab4_tm_none_kernel(tc, tab, w, offs, out):
 
         out_view = out.rearrange("(j p) n -> p j n", p=P)
 
+        def empty_bank(g, b, copy, staging):
+            js, acc = banks[GROUPS[g][0]][b]
+            copy(out=staging, in_=acc[:])
+
+        def staging_in(spent, rows, width):
+            flat = raw[spent][:].rearrange("p j c -> p (j c)")
+            return flat[:, 0 : rows * width].rearrange("p (j c) -> p j c", j=rows)
+
         def finish(g, copies, spent=None):
             c0, width, parted = GROUPS[g]
             if spent is None:
                 staged = keep.tile([P, J_TILES, width], F32, name=f"result{c0}", align_bytes=64)
                 result = staged[:]
             else:
-                result = raw[spent][:, 0:J_TILES, 0:width]
-            for (js, acc), copy in zip(banks[c0], copies):
-                copy(out=result[:, js[0] : js[-1] + 1, :], in_=acc[:])
+                result = staging_in(spent, J_TILES, width)
+            for b, copy in enumerate(copies):
+                js = banks[c0][b][0]
+                empty_bank(g, b, copy, result[:, js[0] : js[-1] + 1, :])
             nc.sync.dma_start(out=out_view[:, :, c0 : c0 + width], in_=result)
+
+        def finish_bank(g, j, copy, spent):
+            c0, width, parted = GROUPS[g]
+            result = staging_in(spent, 1, width)
+            empty_bank(g, j, copy, result)
+            nc.sync.dma_start(out=out_view[:, j : j + 1, c0 : c0 + width], in_=result)
 
         on_vector, on_scalar = nc.vector.tensor_copy, nc.scalar.copy
         gather(0)
@@ -162,20 +178,23 @@ def tile_list_tab4_tm_none_kernel(tc, tab, w, offs, out):
         cast(3, 0, 512, 288)
         quantise(3, 0, 512)
         multiply(3, 0)
-        cast(2, 512, 512, 288)
-        finish(0, [on_scalar, on_scalar], (2, 512, 512))
-        quantise(2, 512, 512)
-        for g in (1, 2, 3):
-            multiply(2, g)
-        cast(3, 512, 256, 192)
+        cast(2, 512, 512, 320)
+        finish_bank(0, 0, on_scalar, (2, 512, 512))
+        quantise(2, 512, 256)
+        multiply(2, 1)
+        cast(3, 512, 256, 160)
+        finish_bank(0, 1, on_scalar, (3, 512, 256))
+        quantise(2, 768, 256)
+        multiply(2, 2)
+        multiply(2, 3)
         quantise(3, 512, 256)
         multiply(3, 1)
-        cast(3, 768, 128, 80)
-        cast(3, 896, 128, 80)
+        cast(3, 768, 128, 128)
+        cast(3, 896, 128, 128)
+        finish(1, [on_scalar])
         quantise(3, 768, 128)
         multiply(3, 2)
         quantise(3, 896, 128)
         multiply(3, 3)
-        finish(1, [on_scalar])
-        finish(2, [on_vector])
+        finish(2, [on_scalar])
         finish(3, [on_vector, on_scalar])

@@ -22,7 +22,7 @@ PAIRS = PASSES // 2
 J_TILES = S // P
 WORD_BYTES = P * T * 4
 
-GROUPS = ((0, 512, True), (512, 256, False), (768, 128, False), (896, 128, True))
+GROUPS = ((0, 512, True), (512, 256, False), (768, 128, True), (896, 128, True))
 PLAN = ((0, 0, 1024), (1, 0, 1024), (2, 0, 512), (3, 0, 512), (2, 512, 512), (3, 512, 256), (3, 768, 256))
 N_STEP = 128
 
@@ -53,12 +53,14 @@ def tile_list_tab4_tm_none_kernel(tc, tab, w, offs, out):
             for quad in range(4):
                 nc.sync.dma_start(out=view[32 * quad : 32 * quad + 4], in_=rows[4 * quad : 4 * quad + 4])
 
-        raw = {}
+        raw, flats = {}, {}
 
-        def load_w(a, c0, width):
-            piece = keep.tile([P, PACK, width], F32, name=f"raw{a}_{c0}", align_bytes=64)
+        def load_w(a, c0, width, spare=0):
+            flat = keep.tile([P, PACK * width + spare], F32, name=f"raw{a}_{c0}", align_bytes=64)
+            flats[a, c0, width] = flat
+            piece = flat[:, 0 : PACK * width].rearrange("p (j c) -> p j c", j=PACK)
             nc.sync.dma_start(
-                out=piece[:],
+                out=piece,
                 in_=w[a * K_PASS : (a + 1) * K_PASS, c0 : c0 + width].rearrange("(p j) c -> p j c", j=PACK),
             )
             raw[a, c0, width] = piece
@@ -137,17 +139,16 @@ def tile_list_tab4_tm_none_kernel(tc, tab, w, offs, out):
             js, acc = banks[GROUPS[g][0]][b]
             copy(out=staging, in_=acc[:])
 
-        def staging_in(spent, rows, width):
-            flat = raw[spent][:].rearrange("p j c -> p (j c)")
-            return flat[:, 0 : rows * width].rearrange("p (j c) -> p j c", j=rows)
+        def staging_in(spent, rows, width, first=0):
+            return flats[spent][:, first : first + rows * width].rearrange("p (j c) -> p j c", j=rows)
 
-        def finish(g, copies, spent=None):
+        def finish(g, copies, spent=None, first=0):
             c0, width, parted = GROUPS[g]
             if spent is None:
                 staged = keep.tile([P, J_TILES, width], F32, name=f"result{c0}", align_bytes=64)
                 result = staged[:]
             else:
-                result = staging_in(spent, J_TILES, width)
+                result = staging_in(spent, J_TILES, width, first)
             for b, copy in enumerate(copies):
                 js = banks[c0][b][0]
                 empty_bank(g, b, copy, result[:, js[0] : js[-1] + 1, :])
@@ -178,17 +179,21 @@ def tile_list_tab4_tm_none_kernel(tc, tab, w, offs, out):
         cast(3, 0, 512, 288)
         quantise(3, 0, 512)
         multiply(3, 0)
-        cast(2, 512, 512, 320)
+        cast(2, 512, 256, 160)
+        cast(2, 768, 256, 160)
         finish_bank(0, 0, on_scalar, (2, 512, 512))
         quantise(2, 512, 256)
         multiply(2, 1)
-        cast(3, 512, 256, 160)
-        finish_bank(0, 1, on_scalar, (3, 512, 256))
         quantise(2, 768, 256)
         multiply(2, 2)
         multiply(2, 3)
-        quantise(3, 512, 256)
-        multiply(3, 1)
+        cast(3, 512, 128, 80)
+        cast(3, 640, 128, 80)
+        finish_bank(0, 1, on_scalar, (3, 512, 256))
+        quantise(3, 512, 128)
+        multiply(3, 1, 0, 128)
+        quantise(3, 640, 128)
+        multiply(3, 1, 128, 256)
         cast(3, 768, 128, 128)
         cast(3, 896, 128, 128)
         finish(1, [on_scalar])
@@ -196,5 +201,5 @@ def tile_list_tab4_tm_none_kernel(tc, tab, w, offs, out):
         multiply(3, 2)
         quantise(3, 896, 128)
         multiply(3, 3)
-        finish(2, [on_scalar])
+        finish(2, [on_vector, on_scalar])
         finish(3, [on_vector, on_scalar])

@@ -35,9 +35,10 @@ def tile_list_tab4_tm_none_kernel(tc, tab, w, offs, out):
 
         offsets = keep.tile([P, S // 16], U16, name="offsets")
         words = keep.tile([P, PAIRS, T], I32, name="words", align_bytes=64)
-        planes = [keep.tile([P, 2, T], U8, name=f"planes{m}", align_bytes=64) for m in range(PAIRS)]
-        for m in range(PAIRS):
-            nc.vector.memset(planes[m][:].rearrange("p h t -> p (h t)").bitcast(I32), 0)
+        rows = keep.tile([P, T], U8, name="rows", tag="late", align_bytes=64)
+        nc.vector.memset(rows[64:P, :].bitcast(I32), 0)
+        t_scales = keep.tile([P, 2, PAIRS, S], U8, name="t_scales", align_bytes=64)
+        nc.vector.memset(t_scales[:].rearrange("p h m s -> p (h m s)").bitcast(I32), 0)
 
         tab32 = tab.bitcast(I32)
 
@@ -47,16 +48,15 @@ def tile_list_tab4_tm_none_kernel(tc, tab, w, offs, out):
                 in_=tab32[:, 0 : WORD_BYTES // 4].rearrange("m (p t) -> p m t", p=P),
             )
 
-        def load_planes(m):
-            rows = tab32[m, WORD_BYTES // 4 : (WORD_BYTES + 32 * T) // 4].rearrange("(h q t) -> q h t", h=2, q=16)
-            view = planes[m][:].rearrange("p h t -> p (h t)").bitcast(I32).rearrange("p (h t) -> p h t", h=2)
-            for quad in range(4):
-                nc.sync.dma_start(out=view[32 * quad : 32 * quad + 4], in_=rows[4 * quad : 4 * quad + 4])
+        def load_rows(m):
+            src = tab32[m, WORD_BYTES // 4 : (WORD_BYTES + 32 * T) // 4].rearrange("(h q t) -> q h t", h=2, q=16)
+            nc.sync.dma_start(out=rows[m:64:2, :].bitcast(I32), in_=src)
 
         raw, flats = {}, {}
 
-        def load_w(a, c0, width, spare=0):
-            flat = keep.tile([P, PACK * width + spare], F32, name=f"raw{a}_{c0}", align_bytes=64)
+        def load_w(a, c0, width, flat=None):
+            if flat is None:
+                flat = keep.tile([P, PACK * width], F32, name=f"raw{a}_{c0}", align_bytes=64)
             flats[a, c0, width] = flat
             piece = flat[:, 0 : PACK * width].rearrange("p (j c) -> p j c", j=PACK)
             nc.sync.dma_start(
@@ -67,14 +67,12 @@ def tile_list_tab4_tm_none_kernel(tc, tab, w, offs, out):
 
         load_words()
         nc.sync.dma_start(offsets[:], offs)
-        load_planes(0)
-        load_w(*PLAN[0])
-        load_planes(1)
-        for piece_at in PLAN[1:]:
+        load_rows(0)
+        load_rows(1)
+        for piece_at in PLAN[:2]:
             load_w(*piece_at)
 
         t_codes = [keep.tile([P, 2, 2 * S], U8, name=f"t_codes{m}", align_bytes=64) for m in range(PAIRS)]
-        t_scales = keep.tile([P, PASSES, S], U8, name="t_scales", align_bytes=64)
 
         def gather(m):
             picked = keep.tile([P, S], U32, name=f"picked{m}", align_bytes=64)
@@ -84,9 +82,15 @@ def tile_list_tab4_tm_none_kernel(tc, tab, w, offs, out):
                 in_=picked[:].bitcast(U16).rearrange("p (t h) -> p h t", h=2),
             )
 
-        def gather_scales(m):
-            for h in range(2):
-                nc.vector.tensor_copy(t_scales[:, 2 * m + h, :], planes[m][:, h, :].indirect(offsets[:]))
+        def gather_scales():
+            picked = keep.tile([P, S], U8, name="picked_rows", align_bytes=64)
+            nc.vector.tensor_copy(picked[:], rows[:].indirect(offsets[:]))
+            planes = t_scales[:].rearrange("p h m s -> p (h m s)").bitcast(I32)
+            for quad in range(4):
+                nc.sync.dma_start(
+                    out=planes[32 * quad : 32 * quad + 4, :],
+                    in_=picked[16 * quad : 16 * quad + 16, :].bitcast(I32),
+                )
 
         grouped = [keep.tile([P, M, PACK], BF16, name=f"grouped{a}", align_bytes=64) for a in range(PASSES)]
         w_codes = [keep.tile([P, M], U32, name=f"w_codes{a}", align_bytes=64) for a in range(PASSES)]
@@ -126,7 +130,7 @@ def tile_list_tab4_tm_none_kernel(tc, tab, w, offs, out):
                         nc.tensor.matmul_mx(
                             out=acc[:, j - js[0], n : n + step],
                             lhsT=t_codes[a // 2][:, a % 2, 2 * P * j : 2 * P * (j + 1)].bitcast(FP4X4),
-                            lhsT_scale=t_scales[:, a, P * j : P * (j + 1)],
+                            lhsT_scale=t_scales[:, a % 2, a // 2, P * j : P * (j + 1)],
                             rhs=w_codes[a][:, cols].bitcast(FP8X4),
                             rhs_scale=w_scales[a][:, cols],
                             start=(a == 0 and j == js[0] and n == 0),
@@ -161,12 +165,15 @@ def tile_list_tab4_tm_none_kernel(tc, tab, w, offs, out):
             nc.sync.dma_start(out=out_view[:, j : j + 1, c0 : c0 + width], in_=result)
 
         on_vector, on_scalar = nc.vector.tensor_copy, nc.scalar.copy
+        gather_scales()
+        late = keep.tile([P, 2 * PACK * M], F32, name="late", tag="late", align_bytes=64)
+        first = 0
+        for a, c0, width in PLAN[2:]:
+            load_w(a, c0, width, late[:, first : first + PACK * width])
+            first += PACK * width
         gather(0)
-        gather_scales(0)
         gather(1)
         for a in range(2):
-            if a == 1:
-                gather_scales(1)
             for c0 in (0, 512):
                 cast(a, c0, 512, 240)
             for c0 in (0, 512):

@@ -23,7 +23,7 @@ J_TILES = S // P
 WORD_BYTES = P * T * 4
 
 GROUPS = ((0, 512, True), (512, 256, False), (768, 128, True), (896, 128, True))
-PLAN = ((0, 0, 1024), (1, 0, 1024), (2, 0, 512), (3, 0, 512), (2, 512, 512), (3, 512, 256), (3, 768, 256))
+PLAN = ((0, 0, 1024), (1, 0, 1024), (2, 0, 768), (3, 0, 512), (3, 512, 256), (2, 768, 256), (3, 768, 256))
 N_STEP = 128
 
 
@@ -180,30 +180,31 @@ def tile_list_tab4_tm_none_kernel(tc, tab, w, offs, out):
                 quantise(a, c0, 512)
             for g in range(len(GROUPS)):
                 multiply(a, g)
-        cast(2, 0, 512, 240)
-        quantise(2, 0, 512)
+        cast(2, 0, 384, 384)
+        cast(2, 384, 128, 0)
+        cast(2, 512, 256, 0)
+        quantise(2, 0, 256)
+        quantise(2, 256, 256)
         multiply(2, 0)
-        cast(3, 0, 512, 288)
-        quantise(3, 0, 512)
-        multiply(3, 0)
-        cast(2, 512, 256, 160)
-        cast(2, 768, 256, 160)
-        finish_bank(0, 0, on_scalar, (2, 512, 512))
         quantise(2, 512, 256)
         multiply(2, 1)
+        cast(3, 0, 512, 256)
+        quantise(3, 0, 256)
+        multiply(3, 0, 0, 256)
+        quantise(3, 256, 256)
+        multiply(3, 0, 256, 512)
+        cast(3, 512, 256, 128)
+        finish_bank(0, 0, on_scalar, (3, 512, 256))
+        quantise(3, 512, 256)
+        multiply(3, 1)
+        finish_bank(0, 1, on_scalar, (3, 0, 512))
+        cast(2, 768, 256, 256)
+        finish(1, [on_scalar])
         quantise(2, 768, 256)
         multiply(2, 2)
         multiply(2, 3)
-        cast(3, 512, 128, 80)
-        cast(3, 640, 128, 80)
-        finish_bank(0, 1, on_scalar, (3, 512, 256))
-        quantise(3, 512, 128)
-        multiply(3, 1, 0, 128)
-        quantise(3, 640, 128)
-        multiply(3, 1, 128, 256)
         cast(3, 768, 128, 128)
-        cast(3, 896, 128, 128)
-        finish(1, [on_scalar])
+        cast(3, 896, 128, 32)
         quantise(3, 768, 128)
         multiply(3, 2)
         quantise(3, 896, 128)

@@ -23,7 +23,7 @@ J_TILES = S // P
 WORD_BYTES = P * T * 4
 
 GROUPS = ((0, 512, True), (512, 256, False), (768, 128, True), (896, 128, True))
-PLAN = ((0, 0, 1024), (1, 0, 1024), (2, 0, 768), (3, 0, 512), (3, 512, 256), (2, 768, 256), (3, 768, 256))
+PLAN = ((0, 0, 512), (0, 512, 512), (1, 0, 512), (1, 512, 512), (2, 0, 768), (3, 0, 512), (3, 512, 256), (2, 768, 256), (3, 768, 256))
 N_STEP = 128
 
 
@@ -69,7 +69,7 @@ def tile_list_tab4_tm_none_kernel(tc, tab, w, offs, out):
         nc.sync.dma_start(offsets[:], offs)
         load_rows(0)
         load_rows(1)
-        for piece_at in PLAN[:2]:
+        for piece_at in PLAN[:4]:
             load_w(*piece_at)
 
         t_codes = [keep.tile([P, 2, 2 * S], U8, name=f"t_codes{m}", align_bytes=64) for m in range(PAIRS)]
@@ -168,7 +168,7 @@ def tile_list_tab4_tm_none_kernel(tc, tab, w, offs, out):
         gather_scales()
         late = keep.tile([P, 2 * PACK * M], F32, name="late", tag="late", align_bytes=64)
         first = 0
-        for a, c0, width in PLAN[2:]:
+        for a, c0, width in PLAN[4:]:
             load_w(a, c0, width, late[:, first : first + PACK * width])
             first += PACK * width
         gather(0)

@@ -22,9 +22,10 @@ PAIRS = PASSES // 2
 J_TILES = S // P
 WORD_BYTES = P * T * 4
 
-GROUPS = ((0, 512, True), (512, 256, False), (768, 128, True), (896, 128, True))
-PLAN = ((0, 0, 512), (0, 512, 512), (1, 0, 512), (1, 512, 512), (2, 0, 768), (3, 0, 512), (3, 512, 256), (2, 768, 256), (3, 768, 256))
-N_STEP = 128
+GROUPS = ((0, 256, False), (256, 256, False), (512, 256, True), (768, 128, True), (896, 128, True))
+EDGE = 768
+EARLY = ((0, 0, 1024), (1, 0, 1024))
+LATE = ((3, 0, 512), (3, 512, 256), (3, 768, 256))
 
 
 def tile_list_tab4_tm_none_kernel(tc, tab, w, offs, out):
@@ -57,7 +58,7 @@ def tile_list_tab4_tm_none_kernel(tc, tab, w, offs, out):
         def load_w(a, c0, width, flat=None):
             if flat is None:
                 flat = keep.tile([P, PACK * width], F32, name=f"raw{a}_{c0}", align_bytes=64)
-            flats[a, c0, width] = flat
+            flats[a, c0] = flat
             piece = flat[:, 0 : PACK * width].rearrange("p (j c) -> p j c", j=PACK)
             nc.sync.dma_start(
                 out=piece,
@@ -69,7 +70,7 @@ def tile_list_tab4_tm_none_kernel(tc, tab, w, offs, out):
         nc.sync.dma_start(offsets[:], offs)
         load_rows(0)
         load_rows(1)
-        for piece_at in PLAN[:4]:
+        for piece_at in EARLY:
             load_w(*piece_at)
 
         t_codes = [keep.tile([P, 2, 2 * S], U8, name=f"t_codes{m}", align_bytes=64) for m in range(PAIRS)]
@@ -86,7 +87,7 @@ def tile_list_tab4_tm_none_kernel(tc, tab, w, offs, out):
             picked = keep.tile([P, S], U8, name="picked_rows", align_bytes=64)
             nc.vector.tensor_copy(picked[:], rows[:].indirect(offsets[:]))
             planes = t_scales[:].rearrange("p h m s -> p (h m s)").bitcast(I32)
-            for quad in range(4):
+            for quad in (0, 2, 1, 3):
                 nc.sync.dma_start(
                     out=planes[32 * quad : 32 * quad + 4, :],
                     in_=picked[16 * quad : 16 * quad + 16, :].bitcast(I32),
@@ -95,119 +96,115 @@ def tile_list_tab4_tm_none_kernel(tc, tab, w, offs, out):
         grouped = [keep.tile([P, M, PACK], BF16, name=f"grouped{a}", align_bytes=64) for a in range(PASSES)]
         w_codes = [keep.tile([P, M], U32, name=f"w_codes{a}", align_bytes=64) for a in range(PASSES)]
         w_scales = [keep.tile([P, M], U8, name=f"w_scales{a}", align_bytes=64) for a in range(PASSES)]
-        banks = {}
+        banks = []
         for c0, width, parted in GROUPS:
             held = [(j,) for j in range(J_TILES)] if parted else [tuple(range(J_TILES))]
-            banks[c0] = [(js, psum.tile([P, len(js), width], F32, name=f"acc{c0}_{js[0]}")) for js in held]
+            banks.append([(js, psum.tile([P, len(js), width], F32, name=f"acc{c0}_{js[0]}")) for js in held])
 
-        def cast(a, c0, width, share):
-            first, piece = [(f, t) for (b, f, n), t in raw.items() if b == a and f <= c0 < f + n][0]
-            src = piece[:, :, c0 - first : c0 - first + width]
-            dst = grouped[a][:, c0 : c0 + width, :]
-            for copy, cols in ((nc.vector.tensor_copy, slice(0, share)), (nc.scalar.copy, slice(share, width))):
-                if cols.start < cols.stop:
-                    copy(
-                        out=dst[:, cols, :].rearrange("p (c i) j -> p c j i", i=4),
-                        in_=src[:, :, cols].rearrange("p j (c i) -> p c j i", i=4),
-                    )
+        on_vector, on_scalar = nc.vector.tensor_copy, nc.scalar.copy
 
-        def quantise(a, c0, width):
-            cols = slice(c0, c0 + width)
+        def cast(copy, a, lo, hi):
+            first, piece = [(f, t) for (b, f, n), t in raw.items() if b == a and f <= lo < f + n][0]
+            copy(
+                out=grouped[a][:, lo:hi, :].rearrange("p (c i) j -> p c j i", i=4),
+                in_=piece[:, :, lo - first : hi - first].rearrange("p j (c i) -> p c j i", i=4),
+            )
+
+        def quantise(a, lo, hi):
             nc.vector.quantize_mx(
-                out=w_codes[a][:, cols].bitcast(FP8X4),
-                scales=w_scales[a][:, cols],
-                in_=grouped[a][:, cols, :].rearrange("p c j -> p (c j)"),
+                out=w_codes[a][:, lo:hi].bitcast(FP8X4),
+                scales=w_scales[a][:, lo:hi],
+                in_=grouped[a][:, lo:hi, :].rearrange("p c j -> p (c j)"),
             )
 
         def multiply(a, g, lo=0, hi=None):
             c0, width, parted = GROUPS[g]
             hi = width if hi is None else hi
-            step = 512 if hi - lo == 512 else N_STEP
-            for js, acc in banks[c0]:
+            for js, acc in banks[g]:
                 for j in js:
-                    for n in range(lo, hi, step):
-                        cols = slice(c0 + n, c0 + n + step)
-                        nc.tensor.matmul_mx(
-                            out=acc[:, j - js[0], n : n + step],
-                            lhsT=t_codes[a // 2][:, a % 2, 2 * P * j : 2 * P * (j + 1)].bitcast(FP4X4),
-                            lhsT_scale=t_scales[:, a % 2, a // 2, P * j : P * (j + 1)],
-                            rhs=w_codes[a][:, cols].bitcast(FP8X4),
-                            rhs_scale=w_scales[a][:, cols],
-                            start=(a == 0 and j == js[0] and n == 0),
-                            stop=(a == PASSES - 1 and j == js[-1] and n + step == width),
-                        )
+                    cols = slice(c0 + lo, c0 + hi)
+                    nc.tensor.matmul_mx(
+                        out=acc[:, j - js[0], lo:hi],
+                        lhsT=t_codes[a // 2][:, a % 2, 2 * P * j : 2 * P * (j + 1)].bitcast(FP4X4),
+                        lhsT_scale=t_scales[:, a % 2, a // 2, P * j : P * (j + 1)],
+                        rhs=w_codes[a][:, cols].bitcast(FP8X4),
+                        rhs_scale=w_scales[a][:, cols],
+                        start=(a == 0 and j == js[0] and lo == 0),
+                        stop=(a == PASSES - 1 and j == js[-1] and hi == width),
+                    )
 
         out_view = out.rearrange("(j p) n -> p j n", p=P)
 
-        def empty_bank(g, b, copy, staging):
-            js, acc = banks[GROUPS[g][0]][b]
-            copy(out=staging, in_=acc[:])
-
-        def staging_in(spent, rows, width, first=0):
-            return flats[spent][:, first : first + rows * width].rearrange("p (j c) -> p j c", j=rows)
-
-        def finish(g, copies, spent=None, first=0):
+        def finish(g, copies, spent=None, first=0, apart=False):
             c0, width, parted = GROUPS[g]
             if spent is None:
                 staged = keep.tile([P, J_TILES, width], F32, name=f"result{c0}", align_bytes=64)
                 result = staged[:]
             else:
-                result = staging_in(spent, J_TILES, width, first)
-            for b, copy in enumerate(copies):
-                js = banks[c0][b][0]
-                empty_bank(g, b, copy, result[:, js[0] : js[-1] + 1, :])
-            nc.sync.dma_start(out=out_view[:, :, c0 : c0 + width], in_=result)
+                result = flats[spent][:, first : first + J_TILES * width].rearrange("p (j c) -> p j c", j=J_TILES)
+            for (js, acc), copy in zip(banks[g], copies):
+                copy(out=result[:, js[0] : js[-1] + 1, :], in_=acc[:])
+                if apart:
+                    nc.sync.dma_start(
+                        out=out_view[:, js[0] : js[-1] + 1, c0 : c0 + width], in_=result[:, js[0] : js[-1] + 1, :]
+                    )
+            if not apart:
+                nc.sync.dma_start(out=out_view[:, :, c0 : c0 + width], in_=result)
 
-        def finish_bank(g, j, copy, spent):
-            c0, width, parted = GROUPS[g]
-            result = staging_in(spent, 1, width)
-            empty_bank(g, j, copy, result)
-            nc.sync.dma_start(out=out_view[:, j : j + 1, c0 : c0 + width], in_=result)
-
-        on_vector, on_scalar = nc.vector.tensor_copy, nc.scalar.copy
         gather_scales()
         late = keep.tile([P, 2 * PACK * M], F32, name="late", tag="late", align_bytes=64)
-        first = 0
-        for a, c0, width in PLAN[4:]:
+        pass2 = late[:, 0 : PACK * M]
+        pass2_src = w[2 * K_PASS : 3 * K_PASS, :].rearrange("(p j) c -> p (j c)", j=PACK)
+        cut = PACK * M - (M - EDGE)
+        flats[2, 0] = pass2
+        raw[2, 0, M] = pass2.rearrange("p (j c) -> p j c", j=PACK)
+        nc.sync.dma_start(out=pass2[:, 0:cut], in_=pass2_src[:, 0:cut])
+        first = PACK * M
+        for a, c0, width in LATE:
+            if c0 == EDGE:
+                nc.sync.dma_start(out=pass2[:, cut:], in_=pass2_src[:, cut:])
             load_w(a, c0, width, late[:, first : first + PACK * width])
             first += PACK * width
         gather(0)
         gather(1)
         for a in range(2):
             for c0 in (0, 512):
-                cast(a, c0, 512, 240)
+                cast(on_vector, a, c0, c0 + 240)
+                cast(on_scalar, a, c0 + 240, c0 + 512)
             for c0 in (0, 512):
-                quantise(a, c0, 512)
+                quantise(a, c0, c0 + 512)
             for g in range(len(GROUPS)):
                 multiply(a, g)
-        cast(2, 0, 384, 384)
-        cast(2, 384, 128, 0)
-        cast(2, 512, 256, 0)
-        quantise(2, 0, 256)
-        quantise(2, 256, 256)
-        multiply(2, 0)
-        quantise(2, 512, 256)
-        multiply(2, 1)
-        cast(3, 0, 512, 256)
-        quantise(3, 0, 256)
-        multiply(3, 0, 0, 256)
-        quantise(3, 256, 256)
-        multiply(3, 0, 256, 512)
-        cast(3, 512, 256, 128)
-        finish_bank(0, 0, on_scalar, (3, 512, 256))
-        quantise(3, 512, 256)
-        multiply(3, 1)
-        finish_bank(0, 1, on_scalar, (3, 0, 512))
-        cast(2, 768, 256, 256)
-        finish(1, [on_scalar])
-        quantise(2, 768, 256)
-        multiply(2, 2)
-        multiply(2, 3)
-        cast(3, 768, 128, 128)
-        cast(3, 896, 128, 32)
-        quantise(3, 768, 128)
+        cast(on_vector, 2, 0, 256)
+        cast(on_vector, 2, 256, 384)
+        cast(on_scalar, 2, 384, 512)
+        cast(on_scalar, 2, 512, 768)
+        for g in range(3):
+            quantise(2, 256 * g, 256 * (g + 1))
+            multiply(2, g)
+        cast(on_vector, 3, 0, 256)
+        cast(on_vector, 3, 256, 336)
+        cast(on_scalar, 3, 336, 512)
+        for g in range(2):
+            quantise(3, 256 * g, 256 * (g + 1))
+            multiply(3, g)
+        cast(on_vector, 3, 512, 640)
+        cast(on_scalar, 3, 640, 768)
+        finish(0, [on_scalar])
+        quantise(3, 512, 768)
         multiply(3, 2)
-        quantise(3, 896, 128)
-        multiply(3, 3)
+        finish(1, [on_scalar])
+        cast(on_vector, 2, 768, 1024)
         finish(2, [on_vector, on_scalar])
-        finish(3, [on_vector, on_scalar])
+        quantise(2, 768, 1024)
+        multiply(2, 3)
+        multiply(2, 4)
+        cast(on_vector, 3, 768, 896)
+        cast(on_vector, 3, 896, 944)
+        cast(on_scalar, 3, 944, 1024)
+        quantise(3, 768, 896)
+        multiply(3, 3)
+        quantise(3, 896, 1024)
+        multiply(3, 4)
+        finish(3, [on_vector, on_scalar], apart=True)
+        finish(4, [on_vector, on_scalar], apart=True)

@@ -22,7 +22,7 @@ PAIRS = PASSES // 2
 J_TILES = S // P
 WORD_BYTES = P * T * 4
 
-GROUPS = ((0, 256, False), (256, 256, False), (512, 256, True), (768, 128, True), (896, 128, True))
+GROUPS = ((0, 512, True), (512, 256, False), (768, 128, True), (896, 128, True))
 EDGE = 768
 EARLY = ((0, 0, 1024), (1, 0, 1024))
 LATE = ((3, 0, 512), (3, 512, 256), (3, 768, 256))
@@ -151,6 +151,17 @@ def tile_list_tab4_tm_none_kernel(tc, tab, w, offs, out):
             if not apart:
                 nc.sync.dma_start(out=out_view[:, :, c0 : c0 + width], in_=result)
 
+        def finish_by_tile(gs, copies):
+            c0 = GROUPS[gs[0]][0]
+            width = sum(GROUPS[g][1] for g in gs)
+            staged = keep.tile([P, J_TILES, width], F32, name=f"result{c0}", align_bytes=64)
+            for g in gs:
+                cols = slice(GROUPS[g][0] - c0, GROUPS[g][0] - c0 + GROUPS[g][1])
+                for (js, acc), copy in zip(banks[g], copies):
+                    copy(out=staged[:, js[0] : js[-1] + 1, cols], in_=acc[:])
+            for j in range(J_TILES):
+                nc.sync.dma_start(out=out_view[:, j : j + 1, c0 : c0 + width], in_=staged[:, j : j + 1, :])
+
         gather_scales()
         late = keep.tile([P, 2 * PACK * M], F32, name="late", tag="late", align_bytes=64)
         pass2 = late[:, 0 : PACK * M]
@@ -176,35 +187,33 @@ def tile_list_tab4_tm_none_kernel(tc, tab, w, offs, out):
             for g in range(len(GROUPS)):
                 multiply(a, g)
         cast(on_vector, 2, 0, 256)
-        cast(on_vector, 2, 256, 384)
-        cast(on_scalar, 2, 384, 512)
+        cast(on_vector, 2, 256, 448)
+        cast(on_scalar, 2, 448, 512)
         cast(on_scalar, 2, 512, 768)
-        for g in range(3):
-            quantise(2, 256 * g, 256 * (g + 1))
-            multiply(2, g)
+        quantise(2, 0, 256)
+        quantise(2, 256, 512)
+        multiply(2, 0)
+        quantise(2, 512, 768)
+        multiply(2, 1)
         cast(on_vector, 3, 0, 256)
         cast(on_vector, 3, 256, 336)
         cast(on_scalar, 3, 336, 512)
-        for g in range(2):
-            quantise(3, 256 * g, 256 * (g + 1))
-            multiply(3, g)
+        for lo in (0, 256):
+            quantise(3, lo, lo + 256)
+            multiply(3, 0, lo, lo + 256)
         cast(on_vector, 3, 512, 640)
         cast(on_scalar, 3, 640, 768)
-        finish(0, [on_scalar])
         quantise(3, 512, 768)
-        multiply(3, 2)
-        finish(1, [on_scalar])
+        multiply(3, 1)
+        finish(0, [on_scalar, on_scalar], apart=True)
         cast(on_vector, 2, 768, 1024)
-        finish(2, [on_vector, on_scalar])
+        finish(1, [on_scalar])
         quantise(2, 768, 1024)
+        multiply(2, 2)
         multiply(2, 3)
-        multiply(2, 4)
         cast(on_vector, 3, 768, 896)
-        cast(on_vector, 3, 896, 944)
-        cast(on_scalar, 3, 944, 1024)
-        quantise(3, 768, 896)
-        multiply(3, 3)
-        quantise(3, 896, 1024)
-        multiply(3, 4)
-        finish(3, [on_vector, on_scalar], apart=True)
-        finish(4, [on_vector, on_scalar], apart=True)
+        cast(on_vector, 3, 896, 1024)
+        for g in (2, 3):
+            quantise(3, GROUPS[g][0], GROUPS[g][0] + 128)
+            multiply(3, g)
+        finish_by_tile((2, 3), [on_vector, on_scalar])

@@ -151,17 +151,6 @@ def tile_list_tab4_tm_none_kernel(tc, tab, w, offs, out):
             if not apart:
                 nc.sync.dma_start(out=out_view[:, :, c0 : c0 + width], in_=result)
 
-        def finish_by_tile(gs, copies):
-            c0 = GROUPS[gs[0]][0]
-            width = sum(GROUPS[g][1] for g in gs)
-            staged = keep.tile([P, J_TILES, width], F32, name=f"result{c0}", align_bytes=64)
-            for g in gs:
-                cols = slice(GROUPS[g][0] - c0, GROUPS[g][0] - c0 + GROUPS[g][1])
-                for (js, acc), copy in zip(banks[g], copies):
-                    copy(out=staged[:, js[0] : js[-1] + 1, cols], in_=acc[:])
-            for j in range(J_TILES):
-                nc.sync.dma_start(out=out_view[:, j : j + 1, c0 : c0 + width], in_=staged[:, j : j + 1, :])
-
         gather_scales()
         late = keep.tile([P, 2 * PACK * M], F32, name="late", tag="late", align_bytes=64)
         pass2 = late[:, 0 : PACK * M]
@@ -196,24 +185,27 @@ def tile_list_tab4_tm_none_kernel(tc, tab, w, offs, out):
         quantise(2, 512, 768)
         multiply(2, 1)
         cast(on_vector, 3, 0, 256)
-        cast(on_vector, 3, 256, 336)
-        cast(on_scalar, 3, 336, 512)
+        cast(on_vector, 3, 256, 352)
+        cast(on_scalar, 3, 352, 512)
         for lo in (0, 256):
             quantise(3, lo, lo + 256)
             multiply(3, 0, lo, lo + 256)
-        cast(on_vector, 3, 512, 640)
-        cast(on_scalar, 3, 640, 768)
+        cast(on_vector, 3, 512, 608)
+        cast(on_scalar, 3, 608, 768)
         quantise(3, 512, 768)
         multiply(3, 1)
         finish(0, [on_scalar, on_scalar], apart=True)
-        cast(on_vector, 2, 768, 1024)
+        cast(on_vector, 2, 768, 896)
+        cast(on_vector, 2, 896, 1024)
         finish(1, [on_scalar])
-        quantise(2, 768, 1024)
+        quantise(2, 768, 896)
         multiply(2, 2)
-        multiply(2, 3)
         cast(on_vector, 3, 768, 896)
         cast(on_vector, 3, 896, 1024)
+        quantise(3, 768, 896)
+        multiply(3, 2)
+        for a in (2, 3):
+            quantise(a, 896, 1024)
+            multiply(a, 3)
         for g in (2, 3):
-            quantise(3, GROUPS[g][0], GROUPS[g][0] + 128)
-            multiply(3, g)
-        finish_by_tile((2, 3), [on_vector, on_scalar])
+            finish(g, [on_vector, on_scalar], apart=True)

@@ -103,11 +103,11 @@ def tile_list_tab4_tm_none_kernel(tc, tab, w, offs, out):
 
         on_vector, on_scalar = nc.vector.tensor_copy, nc.scalar.copy
 
-        def cast(copy, a, lo, hi):
+        def cast(copy, a, lo, hi, r0=0, r1=PACK):
             first, piece = [(f, t) for (b, f, n), t in raw.items() if b == a and f <= lo < f + n][0]
             copy(
-                out=grouped[a][:, lo:hi, :].rearrange("p (c i) j -> p c j i", i=4),
-                in_=piece[:, :, lo - first : hi - first].rearrange("p j (c i) -> p c j i", i=4),
+                out=grouped[a][:, lo:hi, r0:r1].rearrange("p (c i) j -> p c j i", i=r1 - r0),
+                in_=piece[:, r0:r1, lo - first : hi - first].rearrange("p j (c i) -> p c j i", i=r1 - r0),
             )
 
         def quantise(a, lo, hi):
@@ -176,9 +176,10 @@ def tile_list_tab4_tm_none_kernel(tc, tab, w, offs, out):
             for g in range(len(GROUPS)):
                 multiply(a, g)
         cast(on_vector, 2, 0, 256)
-        cast(on_vector, 2, 256, 448)
-        cast(on_scalar, 2, 448, 512)
+        cast(on_vector, 2, 256, 480)
+        cast(on_scalar, 2, 480, 512)
         cast(on_scalar, 2, 512, 768)
+        cast(on_scalar, 2, 768, 1024, 0, 2)
         quantise(2, 0, 256)
         quantise(2, 256, 512)
         multiply(2, 0)
@@ -195,8 +196,8 @@ def tile_list_tab4_tm_none_kernel(tc, tab, w, offs, out):
         quantise(3, 512, 768)
         multiply(3, 1)
         finish(0, [on_scalar, on_scalar], apart=True)
-        cast(on_vector, 2, 768, 896)
-        cast(on_vector, 2, 896, 1024)
+        cast(on_vector, 2, 768, 896, 2, 4)
+        cast(on_vector, 2, 896, 1024, 2, 4)
         finish(1, [on_scalar])
         quantise(2, 768, 896)
         multiply(2, 2)

@@ -37,7 +37,7 @@ def tile_list_tab4_tm_none_kernel(tc, tab, w, offs, out):
         offsets = keep.tile([P, S // 16], U16, name="offsets")
         words = keep.tile([P, PAIRS, T], I32, name="words", align_bytes=64)
         rows = keep.tile([P, T], U8, name="rows", tag="late", align_bytes=64)
-        nc.vector.memset(rows[64:P, :].bitcast(I32), 0)
+        nc.gpsimd.memset(rows[64:P, :].bitcast(I32), 0)
         t_scales = keep.tile([P, 2, PAIRS, S], U8, name="t_scales", align_bytes=64)
         nc.vector.memset(t_scales[:].rearrange("p h m s -> p (h m s)").bitcast(I32), 0)
 
@@ -73,14 +73,15 @@ def tile_list_tab4_tm_none_kernel(tc, tab, w, offs, out):
         for piece_at in EARLY:
             load_w(*piece_at)
 
-        t_codes = [keep.tile([P, 2, 2 * S], U8, name=f"t_codes{m}", align_bytes=64) for m in range(PAIRS)]
+        t_codes = keep.tile([P, PAIRS, 2, 2 * S], U8, name="t_codes", align_bytes=64)
 
-        def gather(m):
-            picked = keep.tile([P, S], U32, name=f"picked{m}", align_bytes=64)
-            nc.vector.tensor_copy(picked[:], words[:, m, :].bitcast(U32).indirect(offsets[:]))
+        def gather_words():
+            picked = keep.tile([P, PAIRS, S], U32, name="picked_words", align_bytes=64)
+            for m in range(PAIRS):
+                nc.vector.tensor_copy(picked[:, m, :], words[:, m, :].bitcast(U32).indirect(offsets[:]))
             nc.vector.tensor_copy(
-                out=t_codes[m][:].rearrange("p h b -> p (h b)").bitcast(U16).rearrange("p (h t) -> p h t", h=2),
-                in_=picked[:].bitcast(U16).rearrange("p (t h) -> p h t", h=2),
+                out=t_codes[:].rearrange("p m h b -> p (m h b)").bitcast(U16).rearrange("p (m h t) -> p m h t", m=PAIRS, h=2),
+                in_=picked[:].rearrange("p m t -> p (m t)").bitcast(U16).rearrange("p (m t h) -> p m h t", m=PAIRS, h=2),
             )
 
         def gather_scales():
@@ -125,7 +126,7 @@ def tile_list_tab4_tm_none_kernel(tc, tab, w, offs, out):
                     cols = slice(c0 + lo, c0 + hi)
                     nc.tensor.matmul_mx(
                         out=acc[:, j - js[0], lo:hi],
-                        lhsT=t_codes[a // 2][:, a % 2, 2 * P * j : 2 * P * (j + 1)].bitcast(FP4X4),
+                        lhsT=t_codes[:, a // 2, a % 2, 2 * P * j : 2 * P * (j + 1)].bitcast(FP4X4),
                         lhsT_scale=t_scales[:, a % 2, a // 2, P * j : P * (j + 1)],
                         rhs=w_codes[a][:, cols].bitcast(FP8X4),
                         rhs_scale=w_scales[a][:, cols],
@@ -165,23 +166,19 @@ def tile_list_tab4_tm_none_kernel(tc, tab, w, offs, out):
                 nc.sync.dma_start(out=pass2[:, cut:], in_=pass2_src[:, cut:])
             load_w(a, c0, width, late[:, first : first + PACK * width])
             first += PACK * width
-        gather(0)
-        gather(1)
+        gather_words()
+        cast(on_scalar, 0, 0, 1024)
+        cast(on_vector, 1, 0, 512)
+        cast(on_scalar, 1, 512, 1024)
         for a in range(2):
-            for c0 in (0, 512):
-                cast(on_vector, a, c0, c0 + 240)
-                cast(on_scalar, a, c0 + 240, c0 + 512)
-            for c0 in (0, 512):
-                quantise(a, c0, c0 + 512)
+            quantise(a, 0, 1024)
             for g in range(len(GROUPS)):
                 multiply(a, g)
-        cast(on_vector, 2, 0, 256)
-        cast(on_vector, 2, 256, 480)
-        cast(on_scalar, 2, 480, 512)
+        cast(on_vector, 2, 0, 448)
+        cast(on_scalar, 2, 448, 512)
         cast(on_scalar, 2, 512, 768)
         cast(on_scalar, 2, 768, 1024, 0, 2)
-        quantise(2, 0, 256)
-        quantise(2, 256, 512)
+        quantise(2, 0, 512)
         multiply(2, 0)
         quantise(2, 512, 768)
         multiply(2, 1)
@@ -196,17 +193,16 @@ def tile_list_tab4_tm_none_kernel(tc, tab, w, offs, out):
         quantise(3, 512, 768)
         multiply(3, 1)
         finish(0, [on_scalar, on_scalar], apart=True)
-        cast(on_vector, 2, 768, 896, 2, 4)
-        cast(on_vector, 2, 896, 1024, 2, 4)
+        cast(on_vector, 2, 768, 1024, 2, 4)
         finish(1, [on_scalar])
-        quantise(2, 768, 896)
+        quantise(2, 768, 1024)
         multiply(2, 2)
+        multiply(2, 3)
         cast(on_vector, 3, 768, 896)
         cast(on_vector, 3, 896, 1024)
         quantise(3, 768, 896)
         multiply(3, 2)
-        for a in (2, 3):
-            quantise(a, 896, 1024)
-            multiply(a, 3)
+        quantise(3, 896, 1024)
+        multiply(3, 3)
         for g in (2, 3):
             finish(g, [on_vector, on_scalar], apart=True)

@@ -37,9 +37,9 @@ def tile_list_tab4_tm_none_kernel(tc, tab, w, offs, out):
         offsets = keep.tile([P, S // 16], U16, name="offsets")
         words = keep.tile([P, PAIRS, T], I32, name="words", align_bytes=64)
         rows = keep.tile([P, T], U8, name="rows", tag="late", align_bytes=64)
-        nc.gpsimd.memset(rows[64:P, :].bitcast(I32), 0)
+        nc.vector.memset(rows[64:P, :].bitcast(I32), 0)
         t_scales = keep.tile([P, 2, PAIRS, S], U8, name="t_scales", align_bytes=64)
-        nc.vector.memset(t_scales[:].rearrange("p h m s -> p (h m s)").bitcast(I32), 0)
+        nc.gpsimd.memset(t_scales[:].rearrange("p h m s -> p (h m s)").bitcast(I32), 0)
 
         tab32 = tab.bitcast(I32)
 
@@ -168,17 +168,22 @@ def tile_list_tab4_tm_none_kernel(tc, tab, w, offs, out):
             first += PACK * width
         gather_words()
         cast(on_scalar, 0, 0, 1024)
-        cast(on_vector, 1, 0, 512)
-        cast(on_scalar, 1, 512, 1024)
+        cast(on_vector, 1, 0, 640)
+        cast(on_scalar, 1, 640, 1024)
+        quantise(0, 0, 1024)
+        quantise(1, 0, 512)
+        quantise(1, 512, 1024)
         for a in range(2):
-            quantise(a, 0, 1024)
-            for g in range(len(GROUPS)):
+            multiply(a, 0, 0, 256)
+            multiply(a, 0, 256, 512)
+            for g in range(1, len(GROUPS)):
                 multiply(a, g)
         cast(on_vector, 2, 0, 448)
         cast(on_scalar, 2, 448, 512)
         cast(on_scalar, 2, 512, 768)
         cast(on_scalar, 2, 768, 1024, 0, 2)
-        quantise(2, 0, 512)
+        quantise(2, 0, 256)
+        quantise(2, 256, 512)
         multiply(2, 0)
         quantise(2, 512, 768)
         multiply(2, 1)

@@ -22,10 +22,7 @@ PAIRS = PASSES // 2
 J_TILES = S // P
 WORD_BYTES = P * T * 4
 
-GROUPS = ((0, 512, True), (512, 256, False), (768, 128, True), (896, 128, True))
-EDGE = 768
-EARLY = ((0, 0, 1024), (1, 0, 1024))
-LATE = ((3, 0, 512), (3, 512, 256), (3, 768, 256))
+GROUPS = ((0, 256, True), (256, 256, True), (512, 256, True), (768, 128, True), (896, 128, True))
 
 
 def tile_list_tab4_tm_none_kernel(tc, tab, w, offs, out):
@@ -53,25 +50,30 @@ def tile_list_tab4_tm_none_kernel(tc, tab, w, offs, out):
             src = tab32[m, WORD_BYTES // 4 : (WORD_BYTES + 32 * T) // 4].rearrange("(h q t) -> q h t", h=2, q=16)
             nc.sync.dma_start(out=rows[m:64:2, :].bitcast(I32), in_=src)
 
-        raw, flats = {}, {}
+        pieces = {}
 
-        def load_w(a, c0, width, flat=None):
-            if flat is None:
-                flat = keep.tile([P, PACK * width], F32, name=f"raw{a}_{c0}", align_bytes=64)
-            flats[a, c0] = flat
-            piece = flat[:, 0 : PACK * width].rearrange("p (j c) -> p j c", j=PACK)
-            nc.sync.dma_start(
-                out=piece,
-                in_=w[a * K_PASS : (a + 1) * K_PASS, c0 : c0 + width].rearrange("(p j) c -> p j c", j=PACK),
-            )
-            raw[a, c0, width] = piece
+        def source(a):
+            return w[a * K_PASS : (a + 1) * K_PASS, :].rearrange("(p j) c -> p (j c)", j=PACK)
+
+        def load_run(a, room, lo, hi):
+            nc.sync.dma_start(out=room[:, lo:hi], in_=source(a)[:, lo:hi])
+
+        def load_block(a, r0, r1, lo, hi, room):
+            block = room.rearrange("p (j c) -> p j c", j=r1 - r0)
+            nc.sync.dma_start(out=block, in_=source(a).rearrange("p (j c) -> p j c", j=PACK)[:, r0:r1, lo:hi])
+            pieces[a, r0, r1, lo, hi] = block
+
+        def load_pass(a):
+            room = keep.tile([P, PACK * M], F32, name=f"raw{a}", align_bytes=64)
+            load_run(a, room[:], 0, PACK * M)
+            pieces[a, 0, PACK, 0, M] = room[:].rearrange("p (j c) -> p j c", j=PACK)
 
         load_words()
         nc.sync.dma_start(offsets[:], offs)
         load_rows(0)
         load_rows(1)
-        for piece_at in EARLY:
-            load_w(*piece_at)
+        load_pass(0)
+        load_pass(1)
 
         t_codes = keep.tile([P, PAIRS, 2, 2 * S], U8, name="t_codes", align_bytes=64)
 
@@ -98,17 +100,24 @@ def tile_list_tab4_tm_none_kernel(tc, tab, w, offs, out):
         w_codes = [keep.tile([P, M], U32, name=f"w_codes{a}", align_bytes=64) for a in range(PASSES)]
         w_scales = [keep.tile([P, M], U8, name=f"w_scales{a}", align_bytes=64) for a in range(PASSES)]
         banks = []
-        for c0, width, parted in GROUPS:
+
+        def open_banks(g, tags):
+            c0, width, parted = GROUPS[g]
             held = [(j,) for j in range(J_TILES)] if parted else [tuple(range(J_TILES))]
-            banks.append([(js, psum.tile([P, len(js), width], F32, name=f"acc{c0}_{js[0]}")) for js in held])
+            banks.append([(js, psum.tile([P, len(js), width], F32, name=f"acc{c0}_{js[0]}", tag=f"bank{tags}_{js[0]}")) for js in held])
+
+        for g in range(len(GROUPS) - 1):
+            open_banks(g, g)
 
         on_vector, on_scalar = nc.vector.tensor_copy, nc.scalar.copy
 
         def cast(copy, a, lo, hi, r0=0, r1=PACK):
-            first, piece = [(f, t) for (b, f, n), t in raw.items() if b == a and f <= lo < f + n][0]
+            top, first, piece = [
+                (t, f, v) for (b, t, u, f, e), v in pieces.items() if b == a and t <= r0 and r1 <= u and f <= lo and hi <= e
+            ][-1]
             copy(
                 out=grouped[a][:, lo:hi, r0:r1].rearrange("p (c i) j -> p c j i", i=r1 - r0),
-                in_=piece[:, r0:r1, lo - first : hi - first].rearrange("p j (c i) -> p c j i", i=r1 - r0),
+                in_=piece[:, r0 - top : r1 - top, lo - first : hi - first].rearrange("p j (c i) -> p c j i", i=r1 - r0),
             )
 
         def quantise(a, lo, hi):
@@ -135,37 +144,31 @@ def tile_list_tab4_tm_none_kernel(tc, tab, w, offs, out):
                     )
 
         out_view = out.rearrange("(j p) n -> p j n", p=P)
+        results = [keep.tile([P, J_TILES, width], F32, name=f"result{c0}", align_bytes=64) for c0, width, parted in GROUPS]
 
-        def finish(g, copies, spent=None, first=0, apart=False):
+        def empty(g, b, copy):
+            js, acc = banks[g][b]
+            copy(out=results[g][:, js[0] : js[-1] + 1, :], in_=acc[:])
+
+        def store(g, j0=0, j1=J_TILES):
             c0, width, parted = GROUPS[g]
-            if spent is None:
-                staged = keep.tile([P, J_TILES, width], F32, name=f"result{c0}", align_bytes=64)
-                result = staged[:]
-            else:
-                result = flats[spent][:, first : first + J_TILES * width].rearrange("p (j c) -> p j c", j=J_TILES)
-            for (js, acc), copy in zip(banks[g], copies):
-                copy(out=result[:, js[0] : js[-1] + 1, :], in_=acc[:])
-                if apart:
-                    nc.sync.dma_start(
-                        out=out_view[:, js[0] : js[-1] + 1, c0 : c0 + width], in_=result[:, js[0] : js[-1] + 1, :]
-                    )
-            if not apart:
-                nc.sync.dma_start(out=out_view[:, :, c0 : c0 + width], in_=result)
+            nc.sync.dma_start(out=out_view[:, j0:j1, c0 : c0 + width], in_=results[g][:, j0:j1, :])
 
         gather_scales()
-        late = keep.tile([P, 2 * PACK * M], F32, name="late", tag="late", align_bytes=64)
-        pass2 = late[:, 0 : PACK * M]
-        pass2_src = w[2 * K_PASS : 3 * K_PASS, :].rearrange("(p j) c -> p (j c)", j=PACK)
-        cut = PACK * M - (M - EDGE)
-        flats[2, 0] = pass2
-        raw[2, 0, M] = pass2.rearrange("p (j c) -> p j c", j=PACK)
-        nc.sync.dma_start(out=pass2[:, 0:cut], in_=pass2_src[:, 0:cut])
-        first = PACK * M
-        for a, c0, width in LATE:
-            if c0 == EDGE:
-                nc.sync.dma_start(out=pass2[:, cut:], in_=pass2_src[:, cut:])
-            load_w(a, c0, width, late[:, first : first + PACK * width])
-            first += PACK * width
+        late = keep.tile([P, 2 * PACK * M + M], F32, name="late", tag="late", align_bytes=64)
+        rooms = [0]
+
+        def room_for(count):
+            rooms[0] += count
+            return late[:, rooms[0] - count : rooms[0]]
+
+        pass2 = room_for(PACK * M)
+        pieces[2, 0, PACK, 0, M] = pass2.rearrange("p (j c) -> p j c", j=PACK)
+        load_run(2, pass2, 0, 3 * M + 768)
+        load_block(3, 0, 4, 0, 512, room_for(2048))
+        load_block(3, 0, 4, 512, 768, room_for(1024))
+        load_run(2, pass2, 3 * M + 768, 4 * M)
+        load_block(3, 0, 4, 768, 1024, room_for(1024))
         gather_words()
         cast(on_scalar, 0, 0, 1024)
         cast(on_vector, 1, 0, 640)
@@ -174,40 +177,47 @@ def tile_list_tab4_tm_none_kernel(tc, tab, w, offs, out):
         quantise(1, 0, 512)
         quantise(1, 512, 1024)
         for a in range(2):
-            multiply(a, 0, 0, 256)
-            multiply(a, 0, 256, 512)
-            for g in range(1, len(GROUPS)):
+            for g in range(len(GROUPS) - 1):
                 multiply(a, g)
         cast(on_vector, 2, 0, 448)
-        cast(on_scalar, 2, 448, 512)
-        cast(on_scalar, 2, 512, 768)
+        cast(on_scalar, 2, 448, 768)
         cast(on_scalar, 2, 768, 1024, 0, 2)
         quantise(2, 0, 256)
         quantise(2, 256, 512)
-        multiply(2, 0)
         quantise(2, 512, 768)
-        multiply(2, 1)
+        for g in range(3):
+            multiply(2, g)
         cast(on_vector, 3, 0, 256)
         cast(on_vector, 3, 256, 352)
         cast(on_scalar, 3, 352, 512)
-        for lo in (0, 256):
-            quantise(3, lo, lo + 256)
-            multiply(3, 0, lo, lo + 256)
+        for g in range(2):
+            quantise(3, 256 * g, 256 * g + 256)
+            multiply(3, g)
         cast(on_vector, 3, 512, 608)
         cast(on_scalar, 3, 608, 768)
         quantise(3, 512, 768)
-        multiply(3, 1)
-        finish(0, [on_scalar, on_scalar], apart=True)
+        multiply(3, 2)
+        for g in range(3):
+            for j in range(J_TILES):
+                empty(g, j, on_scalar)
+                store(g, j, j + 1)
+        open_banks(4, 0)
+        multiply(0, 4)
+        multiply(1, 4)
         cast(on_vector, 2, 768, 1024, 2, 4)
-        finish(1, [on_scalar])
         quantise(2, 768, 1024)
-        multiply(2, 2)
         multiply(2, 3)
+        multiply(2, 4)
         cast(on_vector, 3, 768, 896)
         cast(on_vector, 3, 896, 1024)
         quantise(3, 768, 896)
-        multiply(3, 2)
-        quantise(3, 896, 1024)
         multiply(3, 3)
-        for g in (2, 3):
-            finish(g, [on_vector, on_scalar], apart=True)
+        quantise(3, 896, 1024)
+        multiply(3, 4)
+        empty(3, 0, on_vector)
+        store(3, 0, 1)
+        empty(3, 1, on_scalar)
+        store(3, 1, 2)
+        empty(4, 0, on_vector)
+        empty(4, 1, on_scalar)
+        store(4)

@@ -33,8 +33,8 @@ def tile_list_tab4_tm_none_kernel(tc, tab, w, offs, out):
 
         offsets = keep.tile([P, S // 16], U16, name="offsets")
         words = keep.tile([P, PAIRS, T], I32, name="words", align_bytes=64)
-        rows = keep.tile([P, T], U8, name="rows", tag="late", align_bytes=64)
-        nc.vector.memset(rows[64:P, :].bitcast(I32), 0)
+        rows = keep.tile([P, PAIRS, 2, T], U8, name="rows", tag="late", align_bytes=64)
+        nc.gpsimd.memset(rows[:].rearrange("p m h t -> p (m h t)").bitcast(I32), 0)
         t_scales = keep.tile([P, 2, PAIRS, S], U8, name="t_scales", align_bytes=64)
         nc.gpsimd.memset(t_scales[:].rearrange("p h m s -> p (h m s)").bitcast(I32), 0)
 
@@ -48,7 +48,7 @@ def tile_list_tab4_tm_none_kernel(tc, tab, w, offs, out):
 
         def load_rows(m):
             src = tab32[m, WORD_BYTES // 4 : (WORD_BYTES + 32 * T) // 4].rearrange("(h q t) -> q h t", h=2, q=16)
-            nc.sync.dma_start(out=rows[m:64:2, :].bitcast(I32), in_=src)
+            nc.sync.dma_start(out=rows[4:P:8, m].bitcast(I32), in_=src)
 
         pieces = {}
 
@@ -87,14 +87,14 @@ def tile_list_tab4_tm_none_kernel(tc, tab, w, offs, out):
             )
 
         def gather_scales():
-            picked = keep.tile([P, S], U8, name="picked_rows", align_bytes=64)
-            nc.vector.tensor_copy(picked[:], rows[:].indirect(offsets[:]))
+            picked = keep.tile([P, 2, PAIRS, S], U8, name="picked_rows", align_bytes=64)
+            for h in range(2):
+                for m in range(PAIRS):
+                    nc.vector.tensor_copy(picked[:, h, m, :], rows[:, m, h, :].indirect(offsets[:]))
             planes = t_scales[:].rearrange("p h m s -> p (h m s)").bitcast(I32)
-            for quad in (0, 2, 1, 3):
-                nc.sync.dma_start(
-                    out=planes[32 * quad : 32 * quad + 4, :],
-                    in_=picked[16 * quad : 16 * quad + 16, :].bitcast(I32),
-                )
+            spread = picked[:].rearrange("p h m s -> p (h m s)").bitcast(I32)
+            for r in range(4):
+                nc.sync.dma_start(out=planes[r:P:32, :], in_=spread[4 + 8 * r : P : 32, :])
 
         grouped = [keep.tile([P, M, PACK], BF16, name=f"grouped{a}", align_bytes=64) for a in range(PASSES)]
         w_codes = [keep.tile([P, M], U32, name=f"w_codes{a}", align_bytes=64) for a in range(PASSES)]
@@ -174,16 +174,14 @@ def tile_list_tab4_tm_none_kernel(tc, tab, w, offs, out):
         cast(on_vector, 1, 0, 640)
         cast(on_scalar, 1, 640, 1024)
         quantise(0, 0, 1024)
-        quantise(1, 0, 512)
-        quantise(1, 512, 1024)
+        quantise(1, 0, 1024)
         for a in range(2):
             for g in range(len(GROUPS) - 1):
                 multiply(a, g)
-        cast(on_vector, 2, 0, 448)
-        cast(on_scalar, 2, 448, 768)
+        cast(on_vector, 2, 0, 512)
+        cast(on_scalar, 2, 512, 768)
         cast(on_scalar, 2, 768, 1024, 0, 2)
-        quantise(2, 0, 256)
-        quantise(2, 256, 512)
+        quantise(2, 0, 512)
         quantise(2, 512, 768)
         for g in range(3):
             multiply(2, g)
@@ -193,14 +191,22 @@ def tile_list_tab4_tm_none_kernel(tc, tab, w, offs, out):
         for g in range(2):
             quantise(3, 256 * g, 256 * g + 256)
             multiply(3, g)
-        cast(on_vector, 3, 512, 608)
-        cast(on_scalar, 3, 608, 768)
+        cast(on_vector, 3, 512, 624)
+        cast(on_scalar, 3, 624, 768)
         quantise(3, 512, 768)
         multiply(3, 2)
-        for g in range(3):
-            for j in range(J_TILES):
-                empty(g, j, on_scalar)
-                store(g, j, j + 1)
+        empty(0, 0, on_scalar)
+        store(0, 0, 1)
+        empty(0, 1, on_scalar)
+        store(0, 1, 2)
+        empty(1, 0, on_scalar)
+        store(1, 0, 1)
+        empty(1, 1, on_scalar)
+        store(1, 1, 2)
+        empty(2, 0, on_scalar)
+        store(2, 0, 1)
+        empty(2, 1, on_scalar)
+        store(2, 1, 2)
         open_banks(4, 0)
         multiply(0, 4)
         multiply(1, 4)

from contextlib import ExitStack

import concourse.mybir as mybir

K, M, T, S = 2048, 1024, 512, 256
FLOPS = 2 * K * M * S

F32 = mybir.dt.float32
BF16 = mybir.dt.bfloat16
I32 = mybir.dt.int32
U32 = mybir.dt.uint32
U16 = mybir.dt.uint16
U8 = mybir.dt.uint8
FP8X4 = mybir.dt.float8_e4m3fn_x4
FP4X4 = mybir.dt.float4_e2m1fn_x4

P = 128
PACK = 4
K_PASS = P * PACK
PASSES = K // K_PASS
PAIRS = PASSES // 2
J_TILES = S // P
WORD_BYTES = P * T * 4

GROUPS = ((0, 256, True), (256, 256, True), (512, 256, True), (768, 128, True), (896, 128, True))


def tile_list_tab4_tm_none_kernel(tc, tab, w, offs, out):
    nc = tc.nc
    with ExitStack() as ctx:
        keep = ctx.enter_context(tc.tile_pool(name="keep", bufs=1))
        psum = ctx.enter_context(tc.psum_pool(name="psum", bufs=1))

        offsets = keep.tile([P, S // 16], U16, name="offsets")
        words = keep.tile([P, PAIRS, T], I32, name="words", align_bytes=64)
        rows = keep.tile([P, PAIRS, 2, T], U8, name="rows", tag="late", align_bytes=64)
        nc.gpsimd.memset(rows[:].rearrange("p m h t -> p (m h t)").bitcast(I32), 0)
        t_scales = keep.tile([P, 2, PAIRS, S], U8, name="t_scales", align_bytes=64)
        nc.gpsimd.memset(t_scales[:].rearrange("p h m s -> p (h m s)").bitcast(I32), 0)

        tab32 = tab.bitcast(I32)

        def load_words():
            nc.sync.dma_start(
                out=words[:],
                in_=tab32[:, 0 : WORD_BYTES // 4].rearrange("m (p t) -> p m t", p=P),
            )

        def load_rows(m):
            src = tab32[m, WORD_BYTES // 4 : (WORD_BYTES + 32 * T) // 4].rearrange("(h q t) -> q h t", h=2, q=16)
            nc.sync.dma_start(out=rows[4:P:8, m].bitcast(I32), in_=src)

        pieces = {}

        def source(a):
            return w[a * K_PASS : (a + 1) * K_PASS, :].rearrange("(p j) c -> p (j c)", j=PACK)

        def load_run(a, room, lo, hi):
            nc.sync.dma_start(out=room[:, lo:hi], in_=source(a)[:, lo:hi])

        def load_block(a, r0, r1, lo, hi, room):
            block = room.rearrange("p (j c) -> p j c", j=r1 - r0)
            nc.sync.dma_start(out=block, in_=source(a).rearrange("p (j c) -> p j c", j=PACK)[:, r0:r1, lo:hi])
            pieces[a, r0, r1, lo, hi] = block

        def load_pass(a):
            room = keep.tile([P, PACK * M], F32, name=f"raw{a}", align_bytes=64)
            load_run(a, room[:], 0, PACK * M)
            pieces[a, 0, PACK, 0, M] = room[:].rearrange("p (j c) -> p j c", j=PACK)

        load_words()
        nc.sync.dma_start(offsets[:], offs)
        load_rows(0)
        load_rows(1)
        load_pass(0)
        load_pass(1)

        t_codes = keep.tile([P, PAIRS, 2, 2 * S], U8, name="t_codes", align_bytes=64)

        def gather_words():
            picked = keep.tile([P, PAIRS, S], U32, name="picked_words", align_bytes=64)
            for m in range(PAIRS):
                nc.vector.tensor_copy(picked[:, m, :], words[:, m, :].bitcast(U32).indirect(offsets[:]))
            nc.vector.tensor_copy(
                out=t_codes[:].rearrange("p m h b -> p (m h b)").bitcast(U16).rearrange("p (m h t) -> p m h t", m=PAIRS, h=2),
                in_=picked[:].rearrange("p m t -> p (m t)").bitcast(U16).rearrange("p (m t h) -> p m h t", m=PAIRS, h=2),
            )

        def gather_scales():
            picked = keep.tile([P, 2, PAIRS, S], U8, name="picked_rows", align_bytes=64)
            for h in range(2):
                for m in range(PAIRS):
                    nc.vector.tensor_copy(picked[:, h, m, :], rows[:, m, h, :].indirect(offsets[:]))
            planes = t_scales[:].rearrange("p h m s -> p (h m s)").bitcast(I32)
            spread = picked[:].rearrange("p h m s -> p (h m s)").bitcast(I32)
            for r in range(4):
                nc.sync.dma_start(out=planes[r:P:32, :], in_=spread[4 + 8 * r : P : 32, :])

        grouped = [keep.tile([P, M, PACK], BF16, name=f"grouped{a}", align_bytes=64) for a in range(PASSES)]
        w_codes = [keep.tile([P, M], U32, name=f"w_codes{a}", align_bytes=64) for a in range(PASSES)]
        w_scales = [keep.tile([P, M], U8, name=f"w_scales{a}", align_bytes=64) for a in range(PASSES)]
        banks = []

        def open_banks(g, tags):
            c0, width, parted = GROUPS[g]
            held = [(j,) for j in range(J_TILES)] if parted else [tuple(range(J_TILES))]
            banks.append([(js, psum.tile([P, len(js), width], F32, name=f"acc{c0}_{js[0]}", tag=f"bank{tags}_{js[0]}")) for js in held])

        for g in range(len(GROUPS) - 1):
            open_banks(g, g)

        on_vector, on_scalar = nc.vector.tensor_copy, nc.scalar.copy

        def cast(copy, a, lo, hi, r0=0, r1=PACK):
            top, first, piece = [
                (t, f, v) for (b, t, u, f, e), v in pieces.items() if b == a and t <= r0 and r1 <= u and f <= lo and hi <= e
            ][-1]
            copy(
                out=grouped[a][:, lo:hi, r0:r1].rearrange("p (c i) j -> p c j i", i=r1 - r0),
                in_=piece[:, r0 - top : r1 - top, lo - first : hi - first].rearrange("p j (c i) -> p c j i", i=r1 - r0),
            )

        def quantise(a, lo, hi):
            nc.vector.quantize_mx(
                out=w_codes[a][:, lo:hi].bitcast(FP8X4),
                scales=w_scales[a][:, lo:hi],
                in_=grouped[a][:, lo:hi, :].rearrange("p c j -> p (c j)"),
            )

        def multiply(a, g, lo=0, hi=None):
            c0, width, parted = GROUPS[g]
            hi = width if hi is None else hi
            for js, acc in banks[g]:
                for j in js:
                    cols = slice(c0 + lo, c0 + hi)
                    nc.tensor.matmul_mx(
                        out=acc[:, j - js[0], lo:hi],
                        lhsT=t_codes[:, a // 2, a % 2, 2 * P * j : 2 * P * (j + 1)].bitcast(FP4X4),
                        lhsT_scale=t_scales[:, a % 2, a // 2, P * j : P * (j + 1)],
                        rhs=w_codes[a][:, cols].bitcast(FP8X4),
                        rhs_scale=w_scales[a][:, cols],
                        start=(a == 0 and j == js[0] and lo == 0),
                        stop=(a == PASSES - 1 and j == js[-1] and hi == width),
                    )

        out_view = out.rearrange("(j p) n -> p j n", p=P)
        results = [keep.tile([P, J_TILES, width], F32, name=f"result{c0}", align_bytes=64) for c0, width, parted in GROUPS]

        def empty(g, b, copy):
            js, acc = banks[g][b]
            copy(out=results[g][:, js[0] : js[-1] + 1, :], in_=acc[:])

        def store(g, j0=0, j1=J_TILES):
            c0, width, parted = GROUPS[g]
            nc.sync.dma_start(out=out_view[:, j0:j1, c0 : c0 + width], in_=results[g][:, j0:j1, :])

        gather_scales()
        late = keep.tile([P, 2 * PACK * M + M], F32, name="late", tag="late", align_bytes=64)
        rooms = [0]

        def room_for(count):
            rooms[0] += count
            return late[:, rooms[0] - count : rooms[0]]

        pass2 = room_for(PACK * M)
        pieces[2, 0, PACK, 0, M] = pass2.rearrange("p (j c) -> p j c", j=PACK)
        load_run(2, pass2, 0, 3 * M + 768)
        load_block(3, 0, 4, 0, 512, room_for(2048))
        load_block(3, 0, 4, 512, 768, room_for(1024))
        load_run(2, pass2, 3 * M + 768, 4 * M)
        load_block(3, 0, 4, 768, 1024, room_for(1024))
        gather_words()
        cast(on_scalar, 0, 0, 1024)
        cast(on_vector, 1, 0, 640)
        cast(on_scalar, 1, 640, 1024)
        quantise(0, 0, 1024)
        quantise(1, 0, 1024)
        for a in range(2):
            for g in range(len(GROUPS) - 1):
                multiply(a, g)
        cast(on_vector, 2, 0, 512)
        cast(on_scalar, 2, 512, 768)
        cast(on_scalar, 2, 768, 1024, 0, 2)
        quantise(2, 0, 512)
        quantise(2, 512, 768)
        for g in range(3):
            multiply(2, g)
        cast(on_vector, 3, 0, 256)
        cast(on_vector, 3, 256, 352)
        cast(on_scalar, 3, 352, 512)
        for g in range(2):
            quantise(3, 256 * g, 256 * g + 256)
            multiply(3, g)
        cast(on_vector, 3, 512, 624)
        cast(on_scalar, 3, 624, 768)
        quantise(3, 512, 768)
        multiply(3, 2)
        empty(0, 0, on_scalar)
        store(0, 0, 1)
        empty(0, 1, on_scalar)
        store(0, 1, 2)
        empty(1, 0, on_scalar)
        store(1, 0, 1)
        empty(1, 1, on_scalar)
        store(1, 1, 2)
        empty(2, 0, on_scalar)
        store(2, 0, 1)
        empty(2, 1, on_scalar)
        store(2, 1, 2)
        open_banks(4, 0)
        multiply(0, 4)
        multiply(1, 4)
        cast(on_vector, 2, 768, 1024, 2, 4)
        quantise(2, 768, 1024)
        multiply(2, 3)
        multiply(2, 4)
        cast(on_vector, 3, 768, 896)
        cast(on_vector, 3, 896, 1024)
        quantise(3, 768, 896)
        multiply(3, 3)
        quantise(3, 896, 1024)
        multiply(3, 4)
        empty(3, 0, on_vector)
        store(3, 0, 1)
        empty(3, 1, on_scalar)
        store(3, 1, 2)
        empty(4, 0, on_vector)
        empty(4, 1, on_scalar)
        store(4)
